import numpy as np
import ml_dtypes

BF16 = ml_dtypes.bfloat16


def bf(x):
    return np.asarray(x, np.float32).astype(BF16)


def f32(x):
    return np.asarray(x, np.float32)


def f64(x):
    return np.asarray(x).astype(np.float64)


def striped(idx):
    return np.tile(idx.reshape(-1, 16).T, (8, 1))


def rows(idx, k):
    return np.tile(idx, (k, 1))


def look(tab, idx):
    return np.take_along_axis(f64(tab), rows(idx, len(tab)), axis=1)


K, S, D, V, N, M = 128, 2048, 2, 1024, 2048, 512


def setup_inputs():
    return {"tab": f32(np.random.standard_normal((K, S))), "x0": f32(1.0 * np.random.standard_normal((K, V))), "w": bf(np.random.standard_normal((K, M)) / np.sqrt(K)), "b": f32(0.5 * np.random.standard_normal((M, 1))), "offs": striped(np.random.permutation(S)[:N])}


def reference(tab, x0, w, b, offs):
    idx = offs[:16].T.reshape(-1)
    a = (f64(x0) + sum(look(tab, idx[d * V:(d + 1) * V]) for d in range(D))) / (D + 1)
    x = ((f64(x0) - a) ** 2 + sum((look(tab, idx[d * V:(d + 1) * V]) - a) ** 2 for d in range(D))) / (D + 1)
    return np.maximum(f64(w).T @ x + f64(b), 0.0)

@@ -1,0 +1,75 @@
+import math
+
+import concourse.mybir as mybir
+
+F32, BF16, U16 = mybir.dt.float32, mybir.dt.bfloat16, mybir.dt.uint16
+ALU, ACT = mybir.AluOpType, mybir.ActivationFunctionType
+
+R = 128
+S = 2048
+D = 2
+V = 1024
+M = 512
+PIECE = 512
+BLOCKS = M // 128
+PER_COLUMN = 16
+
+FLOPS = 2 * R * M * V
+
+
+def tile_lookup_vari_relu_kernel(tc, tab, x0, w, b, offs, out):
+    nc = tc.nc
+    with (
+        tc.tile_pool(name="held", bufs=1) as held,
+        tc.tile_pool(name="work", bufs=2) as work,
+        tc.psum_pool(name="psum", bufs=8) as psum,
+    ):
+        offsets = held.tile([128, D * V // PER_COLUMN], U16, name="offsets")
+        table = held.tile([R, S], F32, name="table")
+        node = held.tile([R, V], F32, name="node")
+        weights = held.tile([R, M], BF16, name="weights")
+        bias = held.tile([128, BLOCKS], F32, name="bias")
+
+        nc.sync.dma_start(offsets[:], offs)
+        nc.sync.dma_start(table[:, : S // 2], tab[:, : S // 2])
+        nc.scalar.dma_start(table[:, S // 2 :], tab[:, S // 2 :])
+        for j in range(0, V, PIECE):
+            nc.sync.dma_start(node[:, j : j + PIECE], x0[:, j : j + PIECE])
+        nc.scalar.dma_start(weights[:], w)
+        nc.scalar.dma_start(bias[:], b.rearrange("(p c) o -> p (c o)", c=BLOCKS))
+        out_blocks = out.rearrange("(p c) v -> p c v", c=BLOCKS)
+
+        def neighbour(d, j):
+            first = (d * V + j) // PER_COLUMN
+            return table[:].indirect(offsets[:, first : first + PIECE // PER_COLUMN])
+
+        means = []
+        for j in range(0, V, PIECE):
+            partial = work.tile([R, PIECE], F32, name="partial")
+            total = work.tile([R, PIECE], F32, name="total")
+            mean = held.tile([R, PIECE], F32, name=f"mean{j}")
+            nc.vector.tensor_tensor(partial[:], neighbour(0, j), node[:, j : j + PIECE], ALU.add)
+            nc.vector.tensor_tensor(total[:], neighbour(1, j), partial[:], ALU.add)
+            nc.scalar.mul(mean[:], total[:], 1.0 / (D + 1))
+            means.append(mean)
+
+        for j, mean in zip(range(0, V, PIECE), means):
+            deviations = [work.tile([R, PIECE], F32, name=f"deviation{k}") for k in range(D + 1)]
+            squares = [work.tile([R, PIECE], F32, name=f"square{k}") for k in range(D + 1)]
+            nc.vector.tensor_tensor(deviations[D][:], node[:, j : j + PIECE], mean[:], ALU.subtract)
+            for d in range(D):
+                nc.vector.tensor_tensor(deviations[d][:], neighbour(d, j), mean[:], ALU.subtract)
+            for k in (D, 0, 1):
+                nc.scalar.activation(squares[k][:], deviations[k][:], ACT.Square, scale=math.sqrt(1.0 / (D + 1)))
+
+            pair = work.tile([R, PIECE], F32, name="pair")
+            variance = work.tile([R, PIECE], BF16, name="variance")
+            nc.vector.tensor_tensor(pair[:], squares[D][:], squares[0][:], ALU.add)
+            nc.vector.tensor_tensor(variance[:], pair[:], squares[1][:], ALU.add)
+
+            for c in range(BLOCKS):
+                product = psum.tile([128, PIECE], F32, name="product")
+                nc.tensor.matmul(product[:], weights[:, c::BLOCKS], variance[:], start=True, stop=True)
+                layer = work.tile([128, PIECE], F32, name=f"layer{c}")
+                nc.scalar.activation(layer[:], product[:], ACT.Relu, bias=bias[:, c : c + 1])
+                nc.sync.dma_start(out_blocks[:, c, j : j + PIECE], layer[:])

@@ -10,7 +10,8 @@ S = 2048
 D = 2
 V = 1024
 M = 512
-PIECE = 512
+PIECE = 256
+PIECES = V // PIECE
 BLOCKS = M // 128
 PER_COLUMN = 16
 
@@ -21,7 +22,7 @@ def tile_lookup_vari_relu_kernel(tc, tab, x0, w, b, offs, out):
     nc = tc.nc
     with (
         tc.tile_pool(name="held", bufs=1) as held,
-        tc.tile_pool(name="work", bufs=2) as work,
+        tc.tile_pool(name="work", bufs=3) as work,
         tc.psum_pool(name="psum", bufs=8) as psum,
     ):
         offsets = held.tile([128, D * V // PER_COLUMN], U16, name="offsets")
@@ -33,43 +34,71 @@ def tile_lookup_vari_relu_kernel(tc, tab, x0, w, b, offs, out):
         nc.sync.dma_start(offsets[:], offs)
         nc.sync.dma_start(table[:, : S // 2], tab[:, : S // 2])
         nc.scalar.dma_start(table[:, S // 2 :], tab[:, S // 2 :])
-        for j in range(0, V, PIECE):
-            nc.sync.dma_start(node[:, j : j + PIECE], x0[:, j : j + PIECE])
-        nc.scalar.dma_start(weights[:], w)
-        nc.scalar.dma_start(bias[:], b.rearrange("(p c) o -> p (c o)", c=BLOCKS))
+        for i in range(PIECES):
+            queue = nc.sync if i % 2 == 0 else nc.scalar
+            queue.dma_start(node[:, i * PIECE : (i + 1) * PIECE], x0[:, i * PIECE : (i + 1) * PIECE])
+        nc.sync.dma_start(weights[:], w)
+        nc.sync.dma_start(bias[:], b.rearrange("(p c) o -> p (c o)", c=BLOCKS))
         out_blocks = out.rearrange("(p c) v -> p c v", c=BLOCKS)
 
-        def neighbour(d, j):
-            first = (d * V + j) // PER_COLUMN
+        def nodes(i):
+            return slice(i * PIECE, (i + 1) * PIECE)
+
+        def neighbour(d, i):
+            first = (d * V + i * PIECE) // PER_COLUMN
             return table[:].indirect(offsets[:, first : first + PIECE // PER_COLUMN])
 
-        means = []
-        for j in range(0, V, PIECE):
-            partial = work.tile([R, PIECE], F32, name="partial")
+        partials, means, squares, pairs = {}, {}, {}, {}
+
+        def add_first_neighbour(i):
+            partials[i] = work.tile([R, PIECE], F32, name="partial")
+            nc.vector.tensor_tensor(partials[i][:], neighbour(0, i), node[:, nodes(i)], ALU.add)
+
+        def take_mean(i):
             total = work.tile([R, PIECE], F32, name="total")
-            mean = held.tile([R, PIECE], F32, name=f"mean{j}")
-            nc.vector.tensor_tensor(partial[:], neighbour(0, j), node[:, j : j + PIECE], ALU.add)
-            nc.vector.tensor_tensor(total[:], neighbour(1, j), partial[:], ALU.add)
-            nc.scalar.mul(mean[:], total[:], 1.0 / (D + 1))
-            means.append(mean)
+            means[i] = work.tile([R, PIECE], F32, name="mean")
+            nc.vector.tensor_tensor(total[:], neighbour(1, i), partials[i][:], ALU.add)
+            nc.scalar.mul(means[i][:], total[:], 1.0 / (D + 1))
 
-        for j, mean in zip(range(0, V, PIECE), means):
-            deviations = [work.tile([R, PIECE], F32, name=f"deviation{k}") for k in range(D + 1)]
-            squares = [work.tile([R, PIECE], F32, name=f"square{k}") for k in range(D + 1)]
-            nc.vector.tensor_tensor(deviations[D][:], node[:, j : j + PIECE], mean[:], ALU.subtract)
-            for d in range(D):
-                nc.vector.tensor_tensor(deviations[d][:], neighbour(d, j), mean[:], ALU.subtract)
-            for k in (D, 0, 1):
-                nc.scalar.activation(squares[k][:], deviations[k][:], ACT.Square, scale=math.sqrt(1.0 / (D + 1)))
+        def square_deviation(i, k):
+            deviation = work.tile([R, PIECE], F32, name=f"deviation{k}")
+            squares[i, k] = work.tile([R, PIECE], F32, name=f"square{k}")
+            minuend = node[:, nodes(i)] if k == 0 else neighbour(k - 1, i)
+            nc.vector.tensor_tensor(deviation[:], minuend, means[i][:], ALU.subtract)
+            nc.scalar.activation(squares[i, k][:], deviation[:], ACT.Square, scale=math.sqrt(1.0 / (D + 1)))
 
-            pair = work.tile([R, PIECE], F32, name="pair")
+        def add_first_squares(i):
+            pairs[i] = work.tile([R, PIECE], F32, name="pair")
+            nc.vector.tensor_tensor(pairs[i][:], squares[i, 0][:], squares[i, 1][:], ALU.add)
+
+        def dense_layer(i):
             variance = work.tile([R, PIECE], BF16, name="variance")
-            nc.vector.tensor_tensor(pair[:], squares[D][:], squares[0][:], ALU.add)
-            nc.vector.tensor_tensor(variance[:], pair[:], squares[1][:], ALU.add)
-
+            nc.vector.tensor_tensor(variance[:], pairs[i][:], squares[i, 2][:], ALU.add)
+            layer = work.tile([128, BLOCKS, PIECE], F32, name="layer")
             for c in range(BLOCKS):
                 product = psum.tile([128, PIECE], F32, name="product")
                 nc.tensor.matmul(product[:], weights[:, c::BLOCKS], variance[:], start=True, stop=True)
-                layer = work.tile([128, PIECE], F32, name=f"layer{c}")
-                nc.scalar.activation(layer[:], product[:], ACT.Relu, bias=bias[:, c : c + 1])
-                nc.sync.dma_start(out_blocks[:, c, j : j + PIECE], layer[:])
+                if i == PIECES - 1 and c % 2 == 1:
+                    nc.vector.tensor_scalar(
+                        layer[:, c], product[:], bias[:, c : c + 1], 0.0, ALU.add, ALU.max
+                    )
+                else:
+                    nc.scalar.activation(layer[:, c], product[:], ACT.Relu, bias=bias[:, c : c + 1])
+                nc.sync.dma_start(out_blocks[:, c, nodes(i)], layer[:, c])
+
+        for step in range(PIECES + 2):
+            ahead, now, behind = step, step - 1, step - 2
+            if ahead < PIECES:
+                add_first_neighbour(ahead)
+            if 0 <= now < PIECES:
+                square_deviation(now, 0)
+            if 0 <= behind:
+                add_first_squares(behind)
+            if ahead < PIECES:
+                take_mean(ahead)
+            if 0 <= now < PIECES:
+                square_deviation(now, 1)
+            if 0 <= behind:
+                dense_layer(behind)
+            if 0 <= now < PIECES:
+                square_deviation(now, 2)

@@ -10,10 +10,11 @@ S = 2048
 D = 2
 V = 1024
 M = 512
-PIECE = 256
-PIECES = V // PIECE
 BLOCKS = M // 128
 PER_COLUMN = 16
+
+PIECE = V // 4
+PIECES = V // PIECE
 
 FLOPS = 2 * R * M * V
 
@@ -23,7 +24,7 @@ def tile_lookup_vari_relu_kernel(tc, tab, x0, w, b, offs, out):
     with (
         tc.tile_pool(name="held", bufs=1) as held,
         tc.tile_pool(name="work", bufs=3) as work,
-        tc.psum_pool(name="psum", bufs=8) as psum,
+        tc.psum_pool(name="psum", bufs=2 * BLOCKS) as psum,
     ):
         offsets = held.tile([128, D * V // PER_COLUMN], U16, name="offsets")
         table = held.tile([R, S], F32, name="table")
@@ -31,13 +32,16 @@ def tile_lookup_vari_relu_kernel(tc, tab, x0, w, b, offs, out):
         weights = held.tile([R, M], BF16, name="weights")
         bias = held.tile([128, BLOCKS], F32, name="bias")
 
+        warm = held.tile([128, 1], F32, name="warm")
+        nc.vector.memset(warm[:], 0.0)
+        nc.scalar.activation(warm[:], warm[:], ACT.Square)
+
         nc.sync.dma_start(offsets[:], offs)
         nc.sync.dma_start(table[:, : S // 2], tab[:, : S // 2])
         nc.scalar.dma_start(table[:, S // 2 :], tab[:, S // 2 :])
-        for i in range(PIECES):
-            queue = nc.sync if i % 2 == 0 else nc.scalar
-            queue.dma_start(node[:, i * PIECE : (i + 1) * PIECE], x0[:, i * PIECE : (i + 1) * PIECE])
-        nc.sync.dma_start(weights[:], w)
+        nc.sync.dma_start(node[:, :PIECE], x0[:, :PIECE])
+        nc.scalar.dma_start(weights[:], w)
+        nc.sync.dma_start(node[:, PIECE:], x0[:, PIECE:])
         nc.sync.dma_start(bias[:], b.rearrange("(p c) o -> p (c o)", c=BLOCKS))
         out_blocks = out.rearrange("(p c) v -> p c v", c=BLOCKS)
 
@@ -48,7 +52,7 @@ def tile_lookup_vari_relu_kernel(tc, tab, x0, w, b, offs, out):
             first = (d * V + i * PIECE) // PER_COLUMN
             return table[:].indirect(offsets[:, first : first + PIECE // PER_COLUMN])
 
-        partials, means, squares, pairs = {}, {}, {}, {}
+        partials, means, deviations, squares, products = {}, {}, {}, {}, {}
 
         def add_first_neighbour(i):
             partials[i] = work.tile([R, PIECE], F32, name="partial")
@@ -60,30 +64,38 @@ def tile_lookup_vari_relu_kernel(tc, tab, x0, w, b, offs, out):
             nc.vector.tensor_tensor(total[:], neighbour(1, i), partials[i][:], ALU.add)
             nc.scalar.mul(means[i][:], total[:], 1.0 / (D + 1))
 
-        def square_deviation(i, k):
-            deviation = work.tile([R, PIECE], F32, name=f"deviation{k}")
-            squares[i, k] = work.tile([R, PIECE], F32, name=f"square{k}")
-            minuend = node[:, nodes(i)] if k == 0 else neighbour(k - 1, i)
-            nc.vector.tensor_tensor(deviation[:], minuend, means[i][:], ALU.subtract)
-            nc.scalar.activation(squares[i, k][:], deviation[:], ACT.Square, scale=math.sqrt(1.0 / (D + 1)))
+        def deviate(i, d):
+            deviations[i, d] = work.tile([R, PIECE], F32, name=f"deviation{d}")
+            nc.vector.tensor_tensor(deviations[i, d][:], neighbour(d, i), means[i][:], ALU.subtract)
 
-        def add_first_squares(i):
-            pairs[i] = work.tile([R, PIECE], F32, name="pair")
-            nc.vector.tensor_tensor(pairs[i][:], squares[i, 0][:], squares[i, 1][:], ALU.add)
+        def square_second(i):
+            squares[i, "second"] = work.tile([R, PIECE], F32, name="second")
+            nc.scalar.activation(squares[i, "second"][:], deviations[i, 1][:], ACT.Square, scale=math.sqrt(1 / 2))
 
-        def dense_layer(i):
+        def square_mix(i):
+            mix = work.tile([R, PIECE], F32, name="mix")
+            squares[i, "mix"] = work.tile([R, PIECE], F32, name="mix_squared")
+            nc.vector.scalar_tensor_tensor(
+                mix[:], deviations[i, 0][:], 2.0, deviations[i, 1][:], ALU.mult, ALU.add
+            )
+            nc.scalar.activation(squares[i, "mix"][:], mix[:], ACT.Square, scale=math.sqrt(1 / 6))
+
+        def multiply(i):
             variance = work.tile([R, PIECE], BF16, name="variance")
-            nc.vector.tensor_tensor(variance[:], pairs[i][:], squares[i, 2][:], ALU.add)
+            nc.vector.tensor_tensor(variance[:], squares[i, "second"][:], squares[i, "mix"][:], ALU.add)
+            for c in range(BLOCKS):
+                products[i, c] = psum.tile([128, PIECE], F32, name="product")
+                nc.tensor.matmul(products[i, c][:], weights[:, c::BLOCKS], variance[:], start=True, stop=True)
+
+        def finish(i, share):
             layer = work.tile([128, BLOCKS, PIECE], F32, name="layer")
             for c in range(BLOCKS):
-                product = psum.tile([128, PIECE], F32, name="product")
-                nc.tensor.matmul(product[:], weights[:, c::BLOCKS], variance[:], start=True, stop=True)
-                if i == PIECES - 1 and c % 2 == 1:
+                if share and c % 2 == 1:
                     nc.vector.tensor_scalar(
-                        layer[:, c], product[:], bias[:, c : c + 1], 0.0, ALU.add, ALU.max
+                        layer[:, c], products[i, c][:], bias[:, c : c + 1], 0.0, ALU.add, ALU.max
                     )
                 else:
-                    nc.scalar.activation(layer[:, c], product[:], ACT.Relu, bias=bias[:, c : c + 1])
+                    nc.scalar.activation(layer[:, c], products[i, c][:], ACT.Relu, bias=bias[:, c : c + 1])
                 nc.sync.dma_start(out_blocks[:, c, nodes(i)], layer[:, c])
 
         for step in range(PIECES + 2):
@@ -91,14 +103,15 @@ def tile_lookup_vari_relu_kernel(tc, tab, x0, w, b, offs, out):
             if ahead < PIECES:
                 add_first_neighbour(ahead)
             if 0 <= now < PIECES:
-                square_deviation(now, 0)
-            if 0 <= behind:
-                add_first_squares(behind)
+                deviate(now, 0)
             if ahead < PIECES:
                 take_mean(ahead)
             if 0 <= now < PIECES:
-                square_deviation(now, 1)
+                deviate(now, 1)
+                square_second(now)
             if 0 <= behind:
-                dense_layer(behind)
+                multiply(behind)
             if 0 <= now < PIECES:
-                square_deviation(now, 2)
+                square_mix(now)
+            if 0 <= behind:
+                finish(behind, share=step >= PIECES)

import math

import concourse.mybir as mybir

F32, BF16, U16 = mybir.dt.float32, mybir.dt.bfloat16, mybir.dt.uint16
ALU, ACT = mybir.AluOpType, mybir.ActivationFunctionType

R = 128
S = 2048
D = 2
V = 1024
M = 512
BLOCKS = M // 128
PER_COLUMN = 16

PIECE = V // 4
PIECES = V // PIECE

FLOPS = 2 * R * M * V


def tile_lookup_vari_relu_kernel(tc, tab, x0, w, b, offs, out):
    nc = tc.nc
    with (
        tc.tile_pool(name="held", bufs=1) as held,
        tc.tile_pool(name="work", bufs=3) as work,
        tc.psum_pool(name="psum", bufs=2 * BLOCKS) as psum,
    ):
        offsets = held.tile([128, D * V // PER_COLUMN], U16, name="offsets")
        table = held.tile([R, S], F32, name="table")
        node = held.tile([R, V], F32, name="node")
        weights = held.tile([R, M], BF16, name="weights")
        bias = held.tile([128, BLOCKS], F32, name="bias")

        warm = held.tile([128, 1], F32, name="warm")
        nc.vector.memset(warm[:], 0.0)
        nc.scalar.activation(warm[:], warm[:], ACT.Square)

        nc.sync.dma_start(offsets[:], offs)
        nc.sync.dma_start(table[:, : S // 2], tab[:, : S // 2])
        nc.scalar.dma_start(table[:, S // 2 :], tab[:, S // 2 :])
        nc.sync.dma_start(node[:, :PIECE], x0[:, :PIECE])
        nc.scalar.dma_start(weights[:], w)
        nc.sync.dma_start(node[:, PIECE:], x0[:, PIECE:])
        nc.sync.dma_start(bias[:], b.rearrange("(p c) o -> p (c o)", c=BLOCKS))
        out_blocks = out.rearrange("(p c) v -> p c v", c=BLOCKS)

        def nodes(i):
            return slice(i * PIECE, (i + 1) * PIECE)

        def neighbour(d, i):
            first = (d * V + i * PIECE) // PER_COLUMN
            return table[:].indirect(offsets[:, first : first + PIECE // PER_COLUMN])

        partials, means, deviations, squares, products = {}, {}, {}, {}, {}

        def add_first_neighbour(i):
            partials[i] = work.tile([R, PIECE], F32, name="partial")
            nc.vector.tensor_tensor(partials[i][:], neighbour(0, i), node[:, nodes(i)], ALU.add)

        def take_mean(i):
            total = work.tile([R, PIECE], F32, name="total")
            means[i] = work.tile([R, PIECE], F32, name="mean")
            nc.vector.tensor_tensor(total[:], neighbour(1, i), partials[i][:], ALU.add)
            nc.scalar.mul(means[i][:], total[:], 1.0 / (D + 1))

        def deviate(i, d):
            deviations[i, d] = work.tile([R, PIECE], F32, name=f"deviation{d}")
            nc.vector.tensor_tensor(deviations[i, d][:], neighbour(d, i), means[i][:], ALU.subtract)

        def square_second(i):
            squares[i, "second"] = work.tile([R, PIECE], F32, name="second")
            nc.scalar.activation(squares[i, "second"][:], deviations[i, 1][:], ACT.Square, scale=math.sqrt(1 / 2))

        def square_mix(i):
            mix = work.tile([R, PIECE], F32, name="mix")
            squares[i, "mix"] = work.tile([R, PIECE], F32, name="mix_squared")
            nc.vector.scalar_tensor_tensor(
                mix[:], deviations[i, 0][:], 2.0, deviations[i, 1][:], ALU.mult, ALU.add
            )
            nc.scalar.activation(squares[i, "mix"][:], mix[:], ACT.Square, scale=math.sqrt(1 / 6))

        def multiply(i):
            variance = work.tile([R, PIECE], BF16, name="variance")
            nc.vector.tensor_tensor(variance[:], squares[i, "second"][:], squares[i, "mix"][:], ALU.add)
            for c in range(BLOCKS):
                products[i, c] = psum.tile([128, PIECE], F32, name="product")
                nc.tensor.matmul(products[i, c][:], weights[:, c::BLOCKS], variance[:], start=True, stop=True)

        def finish(i, share):
            layer = work.tile([128, BLOCKS, PIECE], F32, name="layer")
            for c in range(BLOCKS):
                if share and c % 2 == 1:
                    nc.vector.tensor_scalar(
                        layer[:, c], products[i, c][:], bias[:, c : c + 1], 0.0, ALU.add, ALU.max
                    )
                else:
                    nc.scalar.activation(layer[:, c], products[i, c][:], ACT.Relu, bias=bias[:, c : c + 1])
                nc.sync.dma_start(out_blocks[:, c, nodes(i)], layer[:, c])

        for step in range(PIECES + 2):
            ahead, now, behind = step, step - 1, step - 2
            if ahead < PIECES:
                add_first_neighbour(ahead)
            if 0 <= now < PIECES:
                deviate(now, 0)
            if ahead < PIECES:
                take_mean(ahead)
            if 0 <= now < PIECES:
                deviate(now, 1)
                square_second(now)
            if 0 <= behind:
                multiply(behind)
            if 0 <= now < PIECES:
                square_mix(now)
            if 0 <= behind:
                finish(behind, share=step >= PIECES)
